import numpy as np, ml_dtypes
CORES = [10,34,74,98]
N = 4
import mx_ref
NC, G = 160, 4
C, C2 = np.float32(0.029), np.float32(0.0145)
BF = ml_dtypes.bfloat16
def cut(t, i, w=512):
    return t[:, w * i:w * i + w]
def tile(rs):
    return np.stack(rs, axis=2).reshape(128, -1).astype(BF)
def layer(w, X):
    out = []
    for i in range(G):
        for t in range(len(X)):
            p = mx_ref.matmul(mx_ref.quantize(cut(w, len(X) * i + t)), X[t])
            z = p if t == 0 else z + p
        out.append(z)
    return out
def act(Z):
    return [np.maximum(z, 0) * C for z in Z]
def act2(Z):
    return [np.maximum(z, 0) * C2 for z in Z]
def setup_inputs(rng):
    def f(*shape):
        return mx_ref.flush((rng.standard_normal(shape, dtype=np.float32) * np.exp2(rng.integers(-2, 3, shape[:-1] + (1,)))).astype(BF))
    return {"x": f(N, 128, 4 * NC), "w1": f(N, 128, G * 512), "w2": f(N, 128, G * 512), "w3": f(N, 128, G * 512), "w4": f(N, 128, 512)}
def setup_inputs_blocks(rng):
    d = setup_inputs(rng)
    for k in ("x", "w1", "w2", "w3", "w4"): d[k] = mx_ref.spread(d[k], rng, 2)
    return d
def setup_inputs_wide(rng):
    d = setup_inputs(rng)
    for k in ("x", "w1", "w2", "w3", "w4"): d[k] = mx_ref.flush((d[k].astype(np.float32) * np.exp2(rng.integers(-4, 5, (N, 1, 1))).astype(np.float32)).astype(BF))
    return d
def reference(x, w1, w2, w3, w4, own=None):
    X = [mx_ref.quantize(x[j]) for j in range(N)]
    t = np.stack([np.stack([tile(act(layer(w1[r], [X[c]]))) for c in range(N)]) for r in range(N)])
    uset = t if own is None else own["t"]
    h = np.zeros((N, 128, 4 * NC), BF)
    for c in range(N):
        for r in range(N):
            P = layer(w2[r], [mx_ref.quantize(uset[r][c])])
            Z = P if r == 0 else [z + p for z, p in zip(Z, P)]
        h[c] = tile(act2(Z))
    use = h if own is None else own["h"]
    H = [mx_ref.quantize(use[j]) for j in range(N)]
    y = np.zeros((N, 128, NC), np.float32)
    for c in range(N):
        for r in range(N):
            p = mx_ref.matmul(mx_ref.quantize(w4[r]), mx_ref.quantize(tile(act(layer(w3[r], [H[c]])))))
            y[c] = p if r == 0 else y[c] + p
    return {"t": t, "h": h, "y": y}

@@ -1,0 +1,341 @@
+from concourse.bass import DstId, RemoteDMATransfer
+from concourse.mybir import dt, AluOpType, ActivationFunctionType as ACT
+
+N, NC, SIM = 4, 160, 112
+STEPS = (1, 3, 2)
+HOST = STEPS[2]
+C1, C2 = 0.029, 0.0145
+SPLIT = 3 * NC
+W3C, W4C = 512, 128
+
+CODES, PLANE = "float8_e4m3fn_x4", "uint8"
+SCRATCH = {
+    "xin": ("sbuf", [128, 4 * NC], "bfloat16"),
+    "w1in": ("sbuf", [128, 2048], "bfloat16"),
+    "w2in": ("sbuf", [128, 2048], "bfloat16"),
+    "w3in": ("sbuf", [128, 2048], "bfloat16"),
+    "w4in": ("sbuf", [128, 512], "bfloat16"),
+    "w1q": ("sbuf", [128, 512], CODES),
+    "w1s": ("sbuf", [128, 512], PLANE),
+    "w2q": ("sbuf", [128, 512], CODES),
+    "w2s": ("sbuf", [128, 512], PLANE),
+    "hq": ("sbuf", [128, NC], CODES),
+    "hs": ("sbuf", [128, NC], PLANE),
+    "ht": ("sbuf", [128, 4 * NC], "bfloat16"),
+    "acc": ("sbuf", [128, 4 * NC], "float32"),
+    "part": ("sbuf", [128, 2 * NC], "float32"),
+    "direct": ("sbuf", [128, N * NC], "float32"),
+    "folded": ("sbuf", [128, SPLIT], "float32"),
+    "land": ("sbuf", [128, N * SPLIT], "float32"),
+    "pre": ("sbuf", [128, SPLIT], "float32"),
+    "yout": ("sbuf", [128, NC], "float32"),
+    "ps": ("psum", [128, 8 * 512], "float32"),
+}
+for _r in range(N):
+    SCRATCH["xq%d" % _r] = ("sbuf", [128, NC], CODES)
+    SCRATCH["xs%d" % _r] = ("sbuf", [128, NC], PLANE)
+    SCRATCH["tt%d" % _r] = ("sbuf", [128, 4 * NC], "bfloat16")
+    SCRATCH["tq%d" % _r] = ("sbuf", [128, NC], CODES)
+    SCRATCH["ts%d" % _r] = ("sbuf", [128, NC], PLANE)
+    SCRATCH["ut%d" % _r] = ("sbuf", [128, 4 * NC], "bfloat16")
+    SCRATCH["uq%d" % _r] = ("sbuf", [128, NC], CODES)
+    SCRATCH["us%d" % _r] = ("sbuf", [128, NC], PLANE)
+    SCRATCH["sp%d" % _r] = ("sbuf", [128, 4 * NC], "float32")
+    SCRATCH["wc%d" % _r] = ("sbuf", [128, W3C + W4C], CODES)
+    SCRATCH["wp%d" % _r] = ("sbuf", [128, W3C + W4C], PLANE)
+
+SEMAPHORES = (["lx", "l1", "l2", "l3", "l4", "st", "qx", "q1", "q2", "q3", "q4", "qh", "hact", "fold", "pre", "total",
+               "sendx", "sendw", "sends", "sendd", "sendf", "rc", "rp", "add0", "add1"]
+              + ["%s%d" % (s, i) for s in ("xa", "qt", "qu", "da", "sa", "wa", "wb") for i in range(N)]
+              + ["%s%d" % (s, b) for s in ("mm", "rd") for b in range(8)])
+
+
+def roles(T, topo, r):
+    own = T.cores[r]
+    others = [c for c in T.cores if c != own]
+    able = [c for c in range(SIM) if topo.chip(c) == topo.chip(own) and c != own and all(topo.may_write(c, o) for o in others)]
+    near = [c for c in able if topo.die(c) == topo.die(own)]
+    far = [c for c in able if topo.die(c) != topo.die(own)]
+    return near[0], far[:2]
+
+
+def on_chip_engines(T, topo, r):
+    fold, _ = roles(T, topo, r)
+    return topo.mask(T.cores[r], fold) & ~topo.mask(T.cores[r], T.cores[(r + 1) % N])
+
+
+def cut_mask(m, k):
+    bits = [b for b in range(m.bit_length()) if m >> b & 1]
+    w = len(bits) // k
+    return [sum(1 << b for b in bits[i * w:(i + 1) * w]) for i in range(k)]
+
+
+def dest(topo, c):
+    rid, pid, _ = topo.addr(c)
+    return DstId(rid=rid, pnc=pid)
+
+
+def copy(topo, dsts, out, in_, mask, rsem):
+    return RemoteDMATransfer(dst_ids=[dest(topo, d) for d in dsts], dma_engine_mask=mask, remote_sem=rsem,
+                             srcs=[in_], dsts=[out] * len(dsts), alu_op=0)
+
+
+def send(g, topo, dsts, out, in_, mask, rsem, lsem):
+    g.remote_dma_fused([copy(topo, dsts, out, in_, mask, rsem)], local_sem=lsem)
+
+
+def rank_program(g, core, T, topo):
+    r = T.rank_of(core)
+    if r is not None:
+        owner(g, core, r, T, topo)
+        return
+    for r in range(N):
+        fold, relay = roles(T, topo, r)
+        if core in relay:
+            relayer(g, core, r, relay.index(core), T, topo)
+        if core == fold:
+            folder(g, core, r, T, topo)
+
+
+def forward(g, core, r, lo, hi, got, wsem, T, topo):
+    others = [T.cores[(r + k) % N] for k in STEPS]
+    mask = topo.mask(core, others[0])
+    codes, plane = T["wc%d" % r][:, lo:hi].bitcast(dt.uint8), T["wp%d" % r][:, lo:hi]
+    g.wait_ge(T.sem.rc, got)
+    send(g, topo, others, codes, codes, mask, wsem, T.sem.sendw)
+    g.wait_ge(T.sem.rp, got)
+    send(g, topo, others, plane, plane, mask, wsem, T.sem.sendw)
+    return 2 * mask.bit_count()
+
+
+def relayer(g, core, r, i, T, topo):
+    half = W3C // 2
+    n = forward(g, core, r, i * half, (i + 1) * half, on_chip_engines(T, topo, r).bit_count() // 2, T.sem["wa%d" % r], T, topo)
+    g.wait_ge(T.sem.sendw, n)
+
+
+def folder(g, core, r, T, topo):
+    nu = on_chip_engines(T, topo, r).bit_count()
+    n = forward(g, core, r, W3C, W3C + W4C, nu, T.sem["wb%d" % r], T, topo)
+    to = T.cores[(r + HOST) % N]
+    src = [(r + HOST - STEPS[0]) % N, r, (r + HOST - STEPS[1]) % N]
+    at = [T.land[:, s * SPLIT:(s + 1) * SPLIT] for s in src]
+    inc = [nu if s == r else topo.mask(T.cores[s], core).bit_count() for s in src]
+    V = g.vector
+    V.wait_ge(T.sem["sa%d" % src[0]], inc[0])
+    V.wait_ge(T.sem["sa%d" % src[1]], inc[1])
+    V.tensor_tensor(T.pre[:], at[0], at[1], AluOpType.add).then_inc(T.sem.pre, 1)
+    V.wait_ge(T.sem.pre, 1)
+    V.wait_ge(T.sem["sa%d" % src[2]], inc[2])
+    V.tensor_tensor(T.pre[:], T.pre[:], at[2], AluOpType.add).then_inc(T.sem.total, 1)
+    g.wait_ge(T.sem.total, 1)
+    mask = topo.mask(core, to)
+    send(g, topo, [to], T.folded[:], T.pre[:], mask, T.sem.fold, T.sem.sendf)
+    g.wait_ge(T.sem.sendw, n)
+    g.wait_ge(T.sem.sendf, mask.bit_count())
+
+
+def owner(g, core, r, T, topo):
+    V, S, P, Y, sem = g.vector, g.scalar, g.tensor, g.sync, T.sem
+    order = [(r + k) % N for k in STEPS]
+    back = [(r - k) % N for k in STEPS]
+    fold, relay = roles(T, topo, r)
+    off = topo.mask(core, T.cores[order[0]])
+    up = on_chip_engines(T, topo, r)
+    ne, nu = off.bit_count(), up.bit_count()
+    wrote, read = [0] * 8, [0] * 8
+
+    def bank(b):
+        return T.ps[:, 512 * b:512 * b + NC]
+
+    def product(b, wq, ws, i, xq, xs, start=True, stop=True):
+        if start and read[b]:
+            P.wait_ge(sem["rd%d" % b], read[b])
+        m = P.matmul_mx(bank(b), wq[:, 128 * i:128 * i + 128], ws[:, 128 * i:128 * i + 128], xq[:], xs[:], start, stop)
+        if stop:
+            wrote[b] += 1
+            m.then_inc(sem["mm%d" % b], 1)
+
+    def turn_of(q, b):
+        read[b] += 1
+        q.wait_ge(sem["mm%d" % b], read[b])
+        return b, read[b]
+
+    def act(q, b, out):
+        mark = turn_of(q, b)
+        if q is S:
+            S.activation(out, bank(b), ACT.Relu, scale=C1).then_inc(sem["rd%d" % b], 1)
+        else:
+            V.tensor_scalar(out, bank(b), 0.0, C1, AluOpType.max, AluOpType.mult).then_inc(sem["rd%d" % b], 1)
+        return mark
+
+    def evict(q, b, out):
+        mark = turn_of(q, b)
+        if q is S:
+            S.activation(out, bank(b), ACT.Copy).then_inc(sem["rd%d" % b], 1)
+        else:
+            V.tensor_copy(out, bank(b)).then_inc(sem["rd%d" % b], 1)
+        return mark
+
+    def after(q, marks):
+        for b, n in marks:
+            q.wait_ge(sem["rd%d" % b], n)
+
+    own_codes, own_plane = T["wc%d" % r], T["wp%d" % r]
+
+    Y.dma_start(T.xin[:], T.x[:]).then_inc(sem.lx, 16)
+    Y.dma_start(T.w1in[:], T.w1[:]).then_inc(sem.l1, 16)
+    Y.dma_start(T.w4in[:], T.w4[:]).then_inc(sem.l4, 16)
+    Y.dma_start(T.w3in[:], T.w3[:]).then_inc(sem.l3, 16)
+    Y.dma_start(T.w2in[:], T.w2[:]).then_inc(sem.l2, 16)
+
+    V.wait_ge(sem.lx, 16)
+    V.quantize_mx(T["xq%d" % r][:], T["xs%d" % r][:], T.xin[:]).then_inc(sem.qx, 1)
+
+    g.wait_ge(sem.qx, 1)
+    xc, xp = T["xq%d" % r][:].bitcast(dt.uint8), T["xs%d" % r][:]
+    for c in back:
+        send(g, topo, [T.cores[c]], xc, xc, off, sem["xa%d" % r], sem.sendx)
+        send(g, topo, [T.cores[c]], xp, xp, off, sem["xa%d" % r], sem.sendx)
+
+    V.wait_ge(sem.l1, 16)
+    V.quantize_mx(T.w1q[:], T.w1s[:], T.w1in[:]).then_inc(sem.q1, 1)
+    P.wait_ge(sem.qx, 1)
+    P.wait_ge(sem.q1, 1)
+    for b in range(4):
+        product(b, T.w1q, T.w1s, b, T["xq%d" % r], T["xs%d" % r])
+    marks = [act(S, b, T["tt%d" % r][:, b:4 * NC:4]) for b in range(4)]
+    V.wait_ge(sem.l4, 16)
+    V.quantize_mx(own_codes[:, W3C:], own_plane[:, W3C:], T.w4in[:]).then_inc(sem.q4, 1)
+    V.wait_ge(sem.l3, 16)
+    V.quantize_mx(own_codes[:, 0:W3C], own_plane[:, 0:W3C], T.w3in[:]).then_inc(sem.q3, 1)
+    after(V, marks)
+    V.quantize_mx(T["tq%d" % r][:], T["ts%d" % r][:], T["tt%d" % r][:]).then_inc(sem["qt%d" % r], 1)
+    V.wait_ge(sem.l2, 16)
+    V.quantize_mx(T.w2q[:], T.w2s[:], T.w2in[:]).then_inc(sem.q2, 1)
+
+    g.wait_ge(sem.q4, 1)
+    view = own_codes[:, W3C:W3C + W4C].bitcast(dt.uint8)
+    send(g, topo, [fold], view, view, up, sem.rc, sem.sendw)
+    view = own_plane[:, W3C:W3C + W4C]
+    send(g, topo, [fold], view, view, up, sem.rp, sem.sendw)
+
+    half, groups = W3C // 2, cut_mask(up, 2)
+    g.wait_ge(sem.q3, 1)
+    views = [own_codes[:, i * half:(i + 1) * half].bitcast(dt.uint8) for i in (0, 1)]
+    g.remote_dma_fused([copy(topo, [relay[i]], views[i], views[i], groups[i], sem.rc) for i in (0, 1)], local_sem=sem.sendw)
+    views = [own_plane[:, i * half:(i + 1) * half] for i in (0, 1)]
+    g.remote_dma_fused([copy(topo, [relay[i]], views[i], views[i], groups[i], sem.rp) for i in (0, 1)], local_sem=sem.sendw)
+
+    def first(c):
+        P.wait_ge(sem["xa%d" % c], 2 * ne)
+        for b in range(4):
+            product(b, T.w1q, T.w1s, b, T["xq%d" % c], T["xs%d" % c])
+
+    def make_t(c):
+        marks = [act((S, V)[b % 2], b, T["tt%d" % c][:, b:4 * NC:4]) for b in range(4)]
+        after(V, marks)
+        V.quantize_mx(T["tq%d" % c][:], T["ts%d" % c][:], T["tt%d" % c][:]).then_inc(sem["qt%d" % c], 1)
+
+    def second(c):
+        P.wait_ge(sem["qt%d" % c], 1)
+        for b in range(4):
+            product(4 + b, T.w2q, T.w2s, b, T["tq%d" % c], T["ts%d" % c])
+
+    def take(c):
+        return [evict((S, V)[b % 2], 4 + b, T["sp%d" % c][:, b * NC:(b + 1) * NC]) for b in range(4)]
+
+    out = {}
+    for c in order:
+        first(c)
+        make_t(c)
+        if c == order[0]:
+            P.wait_ge(sem.q2, 1)
+        second(c)
+        out[c] = take(c)
+    second(r)
+
+    def send_fold(c):
+        after(g, out[c][0:3])
+        f, _ = roles(T, topo, (c - HOST) % N)
+        mask = up if topo.chip(f) == topo.chip(core) else off
+        send(g, topo, [f], T.land[:, r * SPLIT:(r + 1) * SPLIT], T["sp%d" % c][:, 0:SPLIT], mask, sem["sa%d" % r], sem.sends)
+
+    def send_direct(c):
+        after(g, out[c][3:4])
+        send(g, topo, [T.cores[c]], T.direct[:, r * NC:(r + 1) * NC], T["sp%d" % c][:, SPLIT:4 * NC], off, sem["da%d" % r], sem.sendd)
+
+    for c in order:
+        send_fold(c)
+    for c in order:
+        send_direct(c)
+
+    Y.wait_ge(sem.sends, 2 * ne + nu)
+    for c in [r] + order:
+        Y.wait_ge(sem["qt%d" % c], 1)
+        Y.dma_start(T.t[c], T["tt%d" % c][:]).then_inc(sem.st, 16)
+
+    def mine(b, other, out):
+        mark = turn_of(V, 4 + b)
+        V.tensor_tensor(out, bank(4 + b), other, AluOpType.add).then_inc(sem["rd%d" % (4 + b)], 1)
+        return mark
+
+    def came(k):
+        V.wait_ge(sem["da%d" % back[k]], ne)
+        return T.direct[:, back[k] * NC:(back[k] + 1) * NC]
+
+    def act_h(b):
+        S.activation(T.ht[:, b:4 * NC:4], T.acc[:, b * NC:(b + 1) * NC], ACT.Relu, scale=C2).then_inc(sem.hact, 1)
+
+    after(V, [mine(3, came(0), T.part[:, 0:NC])])
+    V.tensor_tensor(T.part[:, NC:2 * NC], T.part[:, 0:NC], came(1), AluOpType.add).then_inc(sem.add0, 1)
+    V.wait_ge(sem.add0, 1)
+    V.tensor_tensor(T.acc[:, 3 * NC:4 * NC], T.part[:, NC:2 * NC], came(2), AluOpType.add).then_inc(sem.add1, 1)
+    S.wait_ge(sem.add1, 1)
+    act_h(3)
+    V.wait_ge(sem.fold, ne)
+    for b in range(3):
+        after(S, [mine(b, T.folded[:, b * NC:(b + 1) * NC], T.acc[:, b * NC:(b + 1) * NC])])
+        act_h(b)
+    V.wait_ge(sem.hact, 4)
+    V.quantize_mx(T.hq[:], T.hs[:], T.ht[:]).then_inc(sem.qh, 1)
+    Y.wait_ge(sem.qh, 1)
+    Y.dma_start(T.h[:], T.ht[:]).then_inc(sem.st, 16)
+
+    turn = [r] + back
+    z = [0]
+
+    def third(c):
+        if c != r:
+            P.wait_ge(sem["wa%d" % c], 4 * ne)
+        banks = []
+        for b in range(4):
+            banks.append(z[0] % 7)
+            z[0] += 1
+            product(banks[b], T["wc%d" % c], T["wp%d" % c], b, T.hq, T.hs)
+        marks = [act((S, V)[b % 2], banks[b], T["ut%d" % c][:, b:4 * NC:4]) for b in range(4)]
+        after(V, marks)
+        V.quantize_mx(T["uq%d" % c][:], T["us%d" % c][:], T["ut%d" % c][:]).then_inc(sem["qu%d" % c], 1)
+
+    def fourth(c):
+        if c != r:
+            P.wait_ge(sem["wb%d" % c], 2 * ne)
+        P.wait_ge(sem["qu%d" % c], 1)
+        product(7, T["wc%d" % c], T["wp%d" % c], 4, T["uq%d" % c], T["us%d" % c], c == turn[0], c == turn[3])
+
+    P.wait_ge(sem.q3, 1)
+    P.wait_ge(sem.q4, 1)
+    P.wait_ge(sem.qh, 1)
+    third(turn[0])
+    for k in (1, 2, 3):
+        third(turn[k])
+        fourth(turn[k - 1])
+    fourth(turn[3])
+    mark = evict(V, 7, T.yout[:])
+    after(Y, [mark])
+    Y.dma_start(T.y[:], T.yout[:]).then_inc(sem.st, 16)
+
+    Y.wait_ge(sem.st, 6 * 16)
+    g.wait_ge(sem.sendx, 6 * ne)
+    g.wait_ge(sem.sendw, 4 * nu)
+    g.wait_ge(sem.sendd, 3 * ne)

@@ -5,8 +5,9 @@ N, NC, SIM = 4, 160, 112
 STEPS = (1, 3, 2)
 HOST = STEPS[2]
 C1, C2 = 0.029, 0.0145
-SPLIT = 3 * NC
+ADDED = 3
 W3C, W4C = 512, 128
+PARTS = ((W3C, W3C + W4C, True), (0, W3C // 2, False), (W3C // 2, W3C, True))
 
 CODES, PLANE = "float8_e4m3fn_x4", "uint8"
 SCRATCH = {
@@ -22,46 +23,62 @@ SCRATCH = {
     "hq": ("sbuf", [128, NC], CODES),
     "hs": ("sbuf", [128, NC], PLANE),
     "ht": ("sbuf", [128, 4 * NC], "bfloat16"),
-    "acc": ("sbuf", [128, 4 * NC], "float32"),
-    "part": ("sbuf", [128, 2 * NC], "float32"),
+    "tt": ("sbuf", [128, N * 4 * NC], "bfloat16"),
+    "ut": ("sbuf", [128, N * 4 * NC], "bfloat16"),
+    "sp": ("sbuf", [128, N * 4 * NC], "float32"),
     "direct": ("sbuf", [128, N * NC], "float32"),
-    "folded": ("sbuf", [128, SPLIT], "float32"),
-    "land": ("sbuf", [128, N * SPLIT], "float32"),
-    "pre": ("sbuf", [128, SPLIT], "float32"),
+    "part": ("sbuf", [128, 2 * NC], "float32"),
+    "folded": ("sbuf", [128, ADDED * NC], "float32"),
+    "acc": ("sbuf", [128, 4 * NC], "float32"),
+    "land": ("sbuf", [128, N * NC], "float32"),
+    "pre": ("sbuf", [128, 2 * NC], "float32"),
     "yout": ("sbuf", [128, NC], "float32"),
     "ps": ("psum", [128, 8 * 512], "float32"),
 }
+for _n in ("x", "t", "u"):
+    SCRATCH[_n + "q"] = ("sbuf", [128, N * NC], CODES)
+    SCRATCH[_n + "s"] = ("sbuf", [128, N * NC], PLANE)
 for _r in range(N):
-    SCRATCH["xq%d" % _r] = ("sbuf", [128, NC], CODES)
-    SCRATCH["xs%d" % _r] = ("sbuf", [128, NC], PLANE)
-    SCRATCH["tt%d" % _r] = ("sbuf", [128, 4 * NC], "bfloat16")
-    SCRATCH["tq%d" % _r] = ("sbuf", [128, NC], CODES)
-    SCRATCH["ts%d" % _r] = ("sbuf", [128, NC], PLANE)
-    SCRATCH["ut%d" % _r] = ("sbuf", [128, 4 * NC], "bfloat16")
-    SCRATCH["uq%d" % _r] = ("sbuf", [128, NC], CODES)
-    SCRATCH["us%d" % _r] = ("sbuf", [128, NC], PLANE)
-    SCRATCH["sp%d" % _r] = ("sbuf", [128, 4 * NC], "float32")
     SCRATCH["wc%d" % _r] = ("sbuf", [128, W3C + W4C], CODES)
     SCRATCH["wp%d" % _r] = ("sbuf", [128, W3C + W4C], PLANE)
 
-SEMAPHORES = (["lx", "l1", "l2", "l3", "l4", "st", "qx", "q1", "q2", "q3", "q4", "qh", "hact", "fold", "pre", "total",
+SEMAPHORES = (["lx", "l1", "l2", "l3", "l4", "st", "qx", "q1", "q2", "q3", "q4", "qh", "hact", "pre", "total",
                "sendx", "sendw", "sends", "sendd", "sendf", "rc", "rp", "add0", "add1"]
-              + ["%s%d" % (s, i) for s in ("xa", "qt", "qu", "da", "sa", "wa", "wb") for i in range(N)]
+              + ["%s%d" % (s, i) for s in ("xa", "qt", "qu", "da", "sa", "wa", "fold", "gc", "gp") for i in range(N)]
               + ["%s%d" % (s, b) for s in ("mm", "rd") for b in range(8)])
 
 
-def roles(T, topo, r):
+def carriers(T, topo, r):
     own = T.cores[r]
-    others = [c for c in T.cores if c != own]
-    able = [c for c in range(SIM) if topo.chip(c) == topo.chip(own) and c != own and all(topo.may_write(c, o) for o in others)]
+    able = [c for c in range(SIM) if topo.chip(c) == topo.chip(own) and c != own
+            and all(topo.may_write(c, T.cores[(r + k) % N]) for k in STEPS)]
     near = [c for c in able if topo.die(c) == topo.die(own)]
     far = [c for c in able if topo.die(c) != topo.die(own)]
-    return near[0], far[:2]
+    return near[:1] + far[:2]
+
+
+def gate(T, topo, core, c):
+    own = T.cores[c]
+    return [o for o in range(SIM) if topo.mates(topo.chip(o), topo.chip(own)) and topo.die(o) == topo.die(core) and topo.may_write(o, own)][0]
+
+
+def stop(T, topo, core, c, gates):
+    if not gates or topo.same_plane(topo.chip(core), topo.chip(T.cores[c])):
+        return T.cores[c]
+    return gate(T, topo, core, c)
+
+
+def adders(T, topo, c):
+    near, far, _ = carriers(T, topo, (c - HOST) % N)
+    return near, far, gate(T, topo, far, c)
 
 
 def on_chip_engines(T, topo, r):
-    fold, _ = roles(T, topo, r)
-    return topo.mask(T.cores[r], fold) & ~topo.mask(T.cores[r], T.cores[(r + 1) % N])
+    return topo.mask(T.cores[r], carriers(T, topo, r)[0]) & ~topo.mask(T.cores[r], T.cores[(r + 1) % N])
+
+
+def part_engines(T, topo, r, core):
+    return on_chip_engines(T, topo, r) if topo.chip(core) == topo.chip(T.cores[r]) else topo.mask(T.cores[r], core)
 
 
 def cut_mask(m, k):
@@ -75,13 +92,12 @@ def dest(topo, c):
     return DstId(rid=rid, pnc=pid)
 
 
-def copy(topo, dsts, out, in_, mask, rsem):
-    return RemoteDMATransfer(dst_ids=[dest(topo, d) for d in dsts], dma_engine_mask=mask, remote_sem=rsem,
-                             srcs=[in_], dsts=[out] * len(dsts), alu_op=0)
+def copy(topo, to, out, in_, mask, rsem):
+    return RemoteDMATransfer(dst_ids=[dest(topo, to)], dma_engine_mask=mask, remote_sem=rsem, srcs=[in_], dsts=[out], alu_op=0)
 
 
-def send(g, topo, dsts, out, in_, mask, rsem, lsem):
-    g.remote_dma_fused([copy(topo, dsts, out, in_, mask, rsem)], local_sem=lsem)
+def send(g, topo, to, out, in_, mask, rsem, lsem):
+    g.remote_dma_fused([copy(topo, to, out, in_, mask, rsem)], local_sem=lsem)
 
 
 def rank_program(g, core, T, topo):
@@ -89,49 +105,72 @@ def rank_program(g, core, T, topo):
     if r is not None:
         owner(g, core, r, T, topo)
         return
+    sent = 0
     for r in range(N):
-        fold, relay = roles(T, topo, r)
-        if core in relay:
-            relayer(g, core, r, relay.index(core), T, topo)
-        if core == fold:
-            folder(g, core, r, T, topo)
+        if core in carriers(T, topo, r):
+            sent += carry(g, core, r, carriers(T, topo, r).index(core), T, topo)
+        for k in STEPS:
+            s = (r - k) % N
+            for i, (lo, hi, gates) in enumerate(PARTS):
+                if stop(T, topo, carriers(T, topo, s)[i], r, gates) == core:
+                    sent += pass_on(g, core, s, r, lo, hi, T, topo)
+    for c in range(N):
+        if core in adders(T, topo, c):
+            add(g, core, c, adders(T, topo, c).index(core), T, topo)
+    if sent:
+        g.wait_ge(T.sem.sendw, sent)
 
 
-def forward(g, core, r, lo, hi, got, wsem, T, topo):
-    others = [T.cores[(r + k) % N] for k in STEPS]
-    mask = topo.mask(core, others[0])
-    codes, plane = T["wc%d" % r][:, lo:hi].bitcast(dt.uint8), T["wp%d" % r][:, lo:hi]
-    g.wait_ge(T.sem.rc, got)
-    send(g, topo, others, codes, codes, mask, wsem, T.sem.sendw)
-    g.wait_ge(T.sem.rp, got)
-    send(g, topo, others, plane, plane, mask, wsem, T.sem.sendw)
-    return 2 * mask.bit_count()
+def weights(T, s, lo, hi):
+    return T["wc%d" % s][:, lo:hi].bitcast(dt.uint8), T["wp%d" % s][:, lo:hi]
 
 
-def relayer(g, core, r, i, T, topo):
-    half = W3C // 2
-    n = forward(g, core, r, i * half, (i + 1) * half, on_chip_engines(T, topo, r).bit_count() // 2, T.sem["wa%d" % r], T, topo)
-    g.wait_ge(T.sem.sendw, n)
-
-
-def folder(g, core, r, T, topo):
+def carry(g, core, r, i, T, topo):
+    lo, hi, gates = PARTS[i]
     nu = on_chip_engines(T, topo, r).bit_count()
-    n = forward(g, core, r, W3C, W3C + W4C, nu, T.sem["wb%d" % r], T, topo)
-    to = T.cores[(r + HOST) % N]
-    src = [(r + HOST - STEPS[0]) % N, r, (r + HOST - STEPS[1]) % N]
-    at = [T.land[:, s * SPLIT:(s + 1) * SPLIT] for s in src]
-    inc = [nu if s == r else topo.mask(T.cores[s], core).bit_count() for s in src]
+    got = nu if i == 0 else nu // 2
+    codes, plane = weights(T, r, lo, hi)
+    n = 0
+    for k in STEPS:
+        c = (r + k) % N
+        to = stop(T, topo, core, c, gates)
+        mask = topo.mask(core, to)
+        there = to == T.cores[c]
+        g.wait_ge(T.sem.rc, got)
+        send(g, topo, to, codes, codes, mask, T.sem[("wa%d" if there else "gc%d") % r], T.sem.sendw)
+        g.wait_ge(T.sem.rp, got)
+        send(g, topo, to, plane, plane, mask, T.sem[("wa%d" if there else "gp%d") % r], T.sem.sendw)
+        n += 2 * mask.bit_count()
+    return n
+
+
+def pass_on(g, core, s, c, lo, hi, T, topo):
+    to = T.cores[c]
+    mask = topo.mask(core, to)
+    n = mask.bit_count()
+    codes, plane = weights(T, s, lo, hi)
+    g.wait_ge(T.sem["gc%d" % s], n)
+    send(g, topo, to, codes, codes, mask, T.sem["wa%d" % s], T.sem.sendw)
+    g.wait_ge(T.sem["gp%d" % s], n)
+    send(g, topo, to, plane, plane, mask, T.sem["wa%d" % s], T.sem.sendw)
+    return 2 * n
+
+
+def add(g, core, c, i, T, topo):
+    to = T.cores[c]
+    src = [(c - k) % N for k in STEPS]
+    at = [T.land[:, s * NC:(s + 1) * NC] for s in src]
+    inc = [part_engines(T, topo, s, core).bit_count() for s in src]
     V = g.vector
     V.wait_ge(T.sem["sa%d" % src[0]], inc[0])
     V.wait_ge(T.sem["sa%d" % src[1]], inc[1])
-    V.tensor_tensor(T.pre[:], at[0], at[1], AluOpType.add).then_inc(T.sem.pre, 1)
+    V.tensor_tensor(T.pre[:, 0:NC], at[0], at[1], AluOpType.add).then_inc(T.sem.pre, 1)
     V.wait_ge(T.sem.pre, 1)
     V.wait_ge(T.sem["sa%d" % src[2]], inc[2])
-    V.tensor_tensor(T.pre[:], T.pre[:], at[2], AluOpType.add).then_inc(T.sem.total, 1)
+    V.tensor_tensor(T.pre[:, NC:2 * NC], T.pre[:, 0:NC], at[2], AluOpType.add).then_inc(T.sem.total, 1)
     g.wait_ge(T.sem.total, 1)
     mask = topo.mask(core, to)
-    send(g, topo, [to], T.folded[:], T.pre[:], mask, T.sem.fold, T.sem.sendf)
-    g.wait_ge(T.sem.sendw, n)
+    send(g, topo, to, T.folded[:, i * NC:(i + 1) * NC], T.pre[:, NC:2 * NC], mask, T.sem["fold%d" % i], T.sem.sendf)
     g.wait_ge(T.sem.sendf, mask.bit_count())
 
 
@@ -139,11 +178,14 @@ def owner(g, core, r, T, topo):
     V, S, P, Y, sem = g.vector, g.scalar, g.tensor, g.sync, T.sem
     order = [(r + k) % N for k in STEPS]
     back = [(r - k) % N for k in STEPS]
-    fold, relay = roles(T, topo, r)
+    carrier = carriers(T, topo, r)
     off = topo.mask(core, T.cores[order[0]])
     up = on_chip_engines(T, topo, r)
     ne, nu = off.bit_count(), up.bit_count()
-    wrote, read = [0] * 8, [0] * 8
+    read = [0] * 8
+
+    def slot(name, c, w=NC):
+        return T[name][:, c * w:(c + 1) * w]
 
     def bank(b):
         return T.ps[:, 512 * b:512 * b + NC]
@@ -151,9 +193,8 @@ def owner(g, core, r, T, topo):
     def product(b, wq, ws, i, xq, xs, start=True, stop=True):
         if start and read[b]:
             P.wait_ge(sem["rd%d" % b], read[b])
-        m = P.matmul_mx(bank(b), wq[:, 128 * i:128 * i + 128], ws[:, 128 * i:128 * i + 128], xq[:], xs[:], start, stop)
+        m = P.matmul_mx(bank(b), wq[:, 128 * i:128 * i + 128], ws[:, 128 * i:128 * i + 128], xq, xs, start, stop)
         if stop:
-            wrote[b] += 1
             m.then_inc(sem["mm%d" % b], 1)
 
     def turn_of(q, b):
@@ -181,7 +222,15 @@ def owner(g, core, r, T, topo):
         for b, n in marks:
             q.wait_ge(sem["rd%d" % b], n)
 
-    own_codes, own_plane = T["wc%d" % r], T["wp%d" % r]
+    def acts(name, c, banks, qs):
+        return [act(q, b, T[name + "t"][:, 4 * NC * c + i:4 * NC * (c + 1):4]) for i, (q, b) in enumerate(zip(qs, banks))]
+
+    def pack(name, c, marks):
+        after(V, marks)
+        V.quantize_mx(slot(name + "q", c), slot(name + "s", c), slot(name + "t", c, 4 * NC)).then_inc(sem["q%s%d" % (name, c)], 1)
+
+    wc, wp = T["wc%d" % r], T["wp%d" % r]
+    LOW, BOTH = (0, 1, 2, 3), (S, V, S, V)
 
     Y.dma_start(T.xin[:], T.x[:]).then_inc(sem.lx, 16)
     Y.dma_start(T.w1in[:], T.w1[:]).then_inc(sem.l1, 16)
@@ -190,90 +239,82 @@ def owner(g, core, r, T, topo):
     Y.dma_start(T.w2in[:], T.w2[:]).then_inc(sem.l2, 16)
 
     V.wait_ge(sem.lx, 16)
-    V.quantize_mx(T["xq%d" % r][:], T["xs%d" % r][:], T.xin[:]).then_inc(sem.qx, 1)
+    V.quantize_mx(slot("xq", r), slot("xs", r), T.xin[:]).then_inc(sem.qx, 1)
 
     g.wait_ge(sem.qx, 1)
-    xc, xp = T["xq%d" % r][:].bitcast(dt.uint8), T["xs%d" % r][:]
-    for c in back:
-        send(g, topo, [T.cores[c]], xc, xc, off, sem["xa%d" % r], sem.sendx)
-        send(g, topo, [T.cores[c]], xp, xp, off, sem["xa%d" % r], sem.sendx)
+    xc, xp = slot("xq", r).bitcast(dt.uint8), slot("xs", r)
+    for k, v in ((2, xp), (0, xc), (0, xp), (1, xc), (1, xp), (2, xc)):
+        send(g, topo, T.cores[back[k]], v, v, off, sem["xa%d" % r], sem.sendx)
+
+    def first(c):
+        if c != r:
+            P.wait_ge(sem["xa%d" % c], 2 * ne)
+        for b in range(4):
+            product(b, T.w1q, T.w1s, b, slot("xq", c), slot("xs", c))
+
+    def second(c):
+        P.wait_ge(sem["qt%d" % c], 1)
+        for b in range(4):
+            product(4 + b, T.w2q, T.w2s, b, slot("tq", c), slot("ts", c))
+
+    out = {}
+
+    def take(c):
+        out[c] = [evict(q, 4 + b, slot("sp", 4 * c + b)) for b, q in enumerate(BOTH)]
 
     V.wait_ge(sem.l1, 16)
     V.quantize_mx(T.w1q[:], T.w1s[:], T.w1in[:]).then_inc(sem.q1, 1)
     P.wait_ge(sem.qx, 1)
     P.wait_ge(sem.q1, 1)
-    for b in range(4):
-        product(b, T.w1q, T.w1s, b, T["xq%d" % r], T["xs%d" % r])
-    marks = [act(S, b, T["tt%d" % r][:, b:4 * NC:4]) for b in range(4)]
+    first(r)
+    marks = acts("t", r, LOW, (S, S, S, S))
     V.wait_ge(sem.l4, 16)
-    V.quantize_mx(own_codes[:, W3C:], own_plane[:, W3C:], T.w4in[:]).then_inc(sem.q4, 1)
+    V.quantize_mx(wc[:, W3C:], wp[:, W3C:], T.w4in[:]).then_inc(sem.q4, 1)
     V.wait_ge(sem.l3, 16)
-    V.quantize_mx(own_codes[:, 0:W3C], own_plane[:, 0:W3C], T.w3in[:]).then_inc(sem.q3, 1)
-    after(V, marks)
-    V.quantize_mx(T["tq%d" % r][:], T["ts%d" % r][:], T["tt%d" % r][:]).then_inc(sem["qt%d" % r], 1)
+    V.quantize_mx(wc[:, 0:W3C], wp[:, 0:W3C], T.w3in[:]).then_inc(sem.q3, 1)
+    pack("t", r, marks)
     V.wait_ge(sem.l2, 16)
     V.quantize_mx(T.w2q[:], T.w2s[:], T.w2in[:]).then_inc(sem.q2, 1)
 
     g.wait_ge(sem.q4, 1)
-    view = own_codes[:, W3C:W3C + W4C].bitcast(dt.uint8)
-    send(g, topo, [fold], view, view, up, sem.rc, sem.sendw)
-    view = own_plane[:, W3C:W3C + W4C]
-    send(g, topo, [fold], view, view, up, sem.rp, sem.sendw)
-
-    half, groups = W3C // 2, cut_mask(up, 2)
+    for v, s in zip(weights(T, r, *PARTS[0][:2]), (sem.rc, sem.rp)):
+        send(g, topo, carrier[0], v, v, up, s, sem.sendw)
+    halves = [(c, m, weights(T, r, *p[:2])) for c, m, p in zip(carrier[1:], cut_mask(up, 2), PARTS[1:])]
     g.wait_ge(sem.q3, 1)
-    views = [own_codes[:, i * half:(i + 1) * half].bitcast(dt.uint8) for i in (0, 1)]
-    g.remote_dma_fused([copy(topo, [relay[i]], views[i], views[i], groups[i], sem.rc) for i in (0, 1)], local_sem=sem.sendw)
-    views = [own_plane[:, i * half:(i + 1) * half] for i in (0, 1)]
-    g.remote_dma_fused([copy(topo, [relay[i]], views[i], views[i], groups[i], sem.rp) for i in (0, 1)], local_sem=sem.sendw)
+    for j, s in enumerate((sem.rc, sem.rp)):
+        g.remote_dma_fused([copy(topo, c, v[j], v[j], m, s) for c, m, v in halves], local_sem=sem.sendw)
 
-    def first(c):
-        P.wait_ge(sem["xa%d" % c], 2 * ne)
-        for b in range(4):
-            product(b, T.w1q, T.w1s, b, T["xq%d" % c], T["xs%d" % c])
-
-    def make_t(c):
-        marks = [act((S, V)[b % 2], b, T["tt%d" % c][:, b:4 * NC:4]) for b in range(4)]
-        after(V, marks)
-        V.quantize_mx(T["tq%d" % c][:], T["ts%d" % c][:], T["tt%d" % c][:]).then_inc(sem["qt%d" % c], 1)
-
-    def second(c):
-        P.wait_ge(sem["qt%d" % c], 1)
-        for b in range(4):
-            product(4 + b, T.w2q, T.w2s, b, T["tq%d" % c], T["ts%d" % c])
-
-    def take(c):
-        return [evict((S, V)[b % 2], 4 + b, T["sp%d" % c][:, b * NC:(b + 1) * NC]) for b in range(4)]
-
-    out = {}
-    for c in order:
-        first(c)
-        make_t(c)
-        if c == order[0]:
-            P.wait_ge(sem.q2, 1)
-        second(c)
-        out[c] = take(c)
+    c1, c2, c3 = order
+    first(c1)
+    pack("t", c1, acts("t", c1, LOW, BOTH))
+    first(c2)
+    P.wait_ge(sem.q2, 1)
+    second(c1)
+    pack("t", c2, acts("t", c2, LOW, BOTH))
+    first(c3)
+    take(c1)
+    second(c2)
+    pack("t", c3, acts("t", c3, LOW, BOTH))
+    take(c2)
+    second(c3)
+    take(c3)
     second(r)
 
-    def send_fold(c):
-        after(g, out[c][0:3])
-        f, _ = roles(T, topo, (c - HOST) % N)
-        mask = up if topo.chip(f) == topo.chip(core) else off
-        send(g, topo, [f], T.land[:, r * SPLIT:(r + 1) * SPLIT], T["sp%d" % c][:, 0:SPLIT], mask, sem["sa%d" % r], sem.sends)
-
-    def send_direct(c):
+    sent = 0
+    for c in order:
+        for i, a in enumerate(adders(T, topo, c)):
+            after(g, out[c][i:i + 1])
+            mask = part_engines(T, topo, r, a)
+            send(g, topo, a, slot("land", r), slot("sp", 4 * c + i), mask, sem["sa%d" % r], sem.sends)
+            sent += mask.bit_count()
+    for c in order:
         after(g, out[c][3:4])
-        send(g, topo, [T.cores[c]], T.direct[:, r * NC:(r + 1) * NC], T["sp%d" % c][:, SPLIT:4 * NC], off, sem["da%d" % r], sem.sendd)
+        send(g, topo, T.cores[c], slot("direct", r), slot("sp", 4 * c + 3), off, sem["da%d" % r], sem.sendd)
 
-    for c in order:
-        send_fold(c)
-    for c in order:
-        send_direct(c)
-
-    Y.wait_ge(sem.sends, 2 * ne + nu)
+    Y.wait_ge(sem.sends, sent)
     for c in [r] + order:
         Y.wait_ge(sem["qt%d" % c], 1)
-        Y.dma_start(T.t[c], T["tt%d" % c][:]).then_inc(sem.st, 16)
+        Y.dma_start(T.t[c], slot("tt", c, 4 * NC)).then_inc(sem.st, 16)
 
     def mine(b, other, out):
         mark = turn_of(V, 4 + b)
@@ -282,20 +323,20 @@ def owner(g, core, r, T, topo):
 
     def came(k):
         V.wait_ge(sem["da%d" % back[k]], ne)
-        return T.direct[:, back[k] * NC:(back[k] + 1) * NC]
+        return slot("direct", back[k])
 
     def act_h(b):
-        S.activation(T.ht[:, b:4 * NC:4], T.acc[:, b * NC:(b + 1) * NC], ACT.Relu, scale=C2).then_inc(sem.hact, 1)
+        S.activation(T.ht[:, b:4 * NC:4], slot("acc", b), ACT.Relu, scale=C2).then_inc(sem.hact, 1)
 
-    after(V, [mine(3, came(0), T.part[:, 0:NC])])
-    V.tensor_tensor(T.part[:, NC:2 * NC], T.part[:, 0:NC], came(1), AluOpType.add).then_inc(sem.add0, 1)
+    after(V, [mine(3, came(0), slot("part", 0))])
+    V.tensor_tensor(slot("part", 1), slot("part", 0), came(1), AluOpType.add).then_inc(sem.add0, 1)
     V.wait_ge(sem.add0, 1)
-    V.tensor_tensor(T.acc[:, 3 * NC:4 * NC], T.part[:, NC:2 * NC], came(2), AluOpType.add).then_inc(sem.add1, 1)
+    V.tensor_tensor(slot("acc", 3), slot("part", 1), came(2), AluOpType.add).then_inc(sem.add1, 1)
     S.wait_ge(sem.add1, 1)
     act_h(3)
-    V.wait_ge(sem.fold, ne)
-    for b in range(3):
-        after(S, [mine(b, T.folded[:, b * NC:(b + 1) * NC], T.acc[:, b * NC:(b + 1) * NC])])
+    for b in range(ADDED):
+        V.wait_ge(sem["fold%d" % b], ne)
+        after(S, [mine(b, slot("folded", b), slot("acc", b))])
         act_h(b)
     V.wait_ge(sem.hact, 4)
     V.quantize_mx(T.hq[:], T.hs[:], T.ht[:]).then_inc(sem.qh, 1)
@@ -307,21 +348,16 @@ def owner(g, core, r, T, topo):
 
     def third(c):
         if c != r:
-            P.wait_ge(sem["wa%d" % c], 4 * ne)
-        banks = []
+            P.wait_ge(sem["wa%d" % c], 2 * ne * len(PARTS))
+        banks = [(z[0] + b) % 7 for b in range(4)]
+        z[0] += 4
         for b in range(4):
-            banks.append(z[0] % 7)
-            z[0] += 1
-            product(banks[b], T["wc%d" % c], T["wp%d" % c], b, T.hq, T.hs)
-        marks = [act((S, V)[b % 2], banks[b], T["ut%d" % c][:, b:4 * NC:4]) for b in range(4)]
-        after(V, marks)
-        V.quantize_mx(T["uq%d" % c][:], T["us%d" % c][:], T["ut%d" % c][:]).then_inc(sem["qu%d" % c], 1)
+            product(banks[b], T["wc%d" % c], T["wp%d" % c], b, T.hq[:], T.hs[:])
+        pack("u", c, acts("u", c, banks, BOTH))
 
     def fourth(c):
-        if c != r:
-            P.wait_ge(sem["wb%d" % c], 2 * ne)
         P.wait_ge(sem["qu%d" % c], 1)
-        product(7, T["wc%d" % c], T["wp%d" % c], 4, T["uq%d" % c], T["us%d" % c], c == turn[0], c == turn[3])
+        product(7, T["wc%d" % c], T["wp%d" % c], 4, slot("uq", c), slot("us", c), c == turn[0], c == turn[3])
 
     P.wait_ge(sem.q3, 1)
     P.wait_ge(sem.q4, 1)
@@ -331,8 +367,7 @@ def owner(g, core, r, T, topo):
         third(turn[k])
         fourth(turn[k - 1])
     fourth(turn[3])
-    mark = evict(V, 7, T.yout[:])
-    after(Y, [mark])
+    after(Y, [evict(V, 7, T.yout[:])])
     Y.dma_start(T.y[:], T.yout[:]).then_inc(sem.st, 16)
 
     Y.wait_ge(sem.st, 6 * 16)

from concourse.bass import DstId, RemoteDMATransfer
from concourse.mybir import dt, AluOpType, ActivationFunctionType as ACT

N, NC, SIM = 4, 160, 112
STEPS = (1, 3, 2)
HOST = STEPS[2]
C1, C2 = 0.029, 0.0145
ADDED = 3
W3C, W4C = 512, 128
PARTS = ((W3C, W3C + W4C, True), (0, W3C // 2, False), (W3C // 2, W3C, True))

CODES, PLANE = "float8_e4m3fn_x4", "uint8"
SCRATCH = {
    "xin": ("sbuf", [128, 4 * NC], "bfloat16"),
    "w1in": ("sbuf", [128, 2048], "bfloat16"),
    "w2in": ("sbuf", [128, 2048], "bfloat16"),
    "w3in": ("sbuf", [128, 2048], "bfloat16"),
    "w4in": ("sbuf", [128, 512], "bfloat16"),
    "w1q": ("sbuf", [128, 512], CODES),
    "w1s": ("sbuf", [128, 512], PLANE),
    "w2q": ("sbuf", [128, 512], CODES),
    "w2s": ("sbuf", [128, 512], PLANE),
    "hq": ("sbuf", [128, NC], CODES),
    "hs": ("sbuf", [128, NC], PLANE),
    "ht": ("sbuf", [128, 4 * NC], "bfloat16"),
    "tt": ("sbuf", [128, N * 4 * NC], "bfloat16"),
    "ut": ("sbuf", [128, N * 4 * NC], "bfloat16"),
    "sp": ("sbuf", [128, N * 4 * NC], "float32"),
    "direct": ("sbuf", [128, N * NC], "float32"),
    "part": ("sbuf", [128, 2 * NC], "float32"),
    "folded": ("sbuf", [128, ADDED * NC], "float32"),
    "acc": ("sbuf", [128, 4 * NC], "float32"),
    "land": ("sbuf", [128, N * NC], "float32"),
    "pre": ("sbuf", [128, 2 * NC], "float32"),
    "yout": ("sbuf", [128, NC], "float32"),
    "ps": ("psum", [128, 8 * 512], "float32"),
}
for _n in ("x", "t", "u"):
    SCRATCH[_n + "q"] = ("sbuf", [128, N * NC], CODES)
    SCRATCH[_n + "s"] = ("sbuf", [128, N * NC], PLANE)
for _r in range(N):
    SCRATCH["wc%d" % _r] = ("sbuf", [128, W3C + W4C], CODES)
    SCRATCH["wp%d" % _r] = ("sbuf", [128, W3C + W4C], PLANE)

SEMAPHORES = (["lx", "l1", "l2", "l3", "l4", "st", "qx", "q1", "q2", "q3", "q4", "qh", "hact", "pre", "total",
               "sendx", "sendw", "sends", "sendd", "sendf", "rc", "rp", "add0", "add1"]
              + ["%s%d" % (s, i) for s in ("xa", "qt", "qu", "da", "sa", "wa", "fold", "gc", "gp") for i in range(N)]
              + ["%s%d" % (s, b) for s in ("mm", "rd") for b in range(8)])


def carriers(T, topo, r):
    own = T.cores[r]
    able = [c for c in range(SIM) if topo.chip(c) == topo.chip(own) and c != own
            and all(topo.may_write(c, T.cores[(r + k) % N]) for k in STEPS)]
    near = [c for c in able if topo.die(c) == topo.die(own)]
    far = [c for c in able if topo.die(c) != topo.die(own)]
    return near[:1] + far[:2]


def gate(T, topo, core, c):
    own = T.cores[c]
    return [o for o in range(SIM) if topo.mates(topo.chip(o), topo.chip(own)) and topo.die(o) == topo.die(core) and topo.may_write(o, own)][0]


def stop(T, topo, core, c, gates):
    if not gates or topo.same_plane(topo.chip(core), topo.chip(T.cores[c])):
        return T.cores[c]
    return gate(T, topo, core, c)


def adders(T, topo, c):
    near, far, _ = carriers(T, topo, (c - HOST) % N)
    return near, far, gate(T, topo, far, c)


def on_chip_engines(T, topo, r):
    return topo.mask(T.cores[r], carriers(T, topo, r)[0]) & ~topo.mask(T.cores[r], T.cores[(r + 1) % N])


def part_engines(T, topo, r, core):
    return on_chip_engines(T, topo, r) if topo.chip(core) == topo.chip(T.cores[r]) else topo.mask(T.cores[r], core)


def cut_mask(m, k):
    bits = [b for b in range(m.bit_length()) if m >> b & 1]
    w = len(bits) // k
    return [sum(1 << b for b in bits[i * w:(i + 1) * w]) for i in range(k)]


def dest(topo, c):
    rid, pid, _ = topo.addr(c)
    return DstId(rid=rid, pnc=pid)


def copy(topo, to, out, in_, mask, rsem):
    return RemoteDMATransfer(dst_ids=[dest(topo, to)], dma_engine_mask=mask, remote_sem=rsem, srcs=[in_], dsts=[out], alu_op=0)


def send(g, topo, to, out, in_, mask, rsem, lsem):
    g.remote_dma_fused([copy(topo, to, out, in_, mask, rsem)], local_sem=lsem)


def rank_program(g, core, T, topo):
    r = T.rank_of(core)
    if r is not None:
        owner(g, core, r, T, topo)
        return
    sent = 0
    for r in range(N):
        if core in carriers(T, topo, r):
            sent += carry(g, core, r, carriers(T, topo, r).index(core), T, topo)
        for k in STEPS:
            s = (r - k) % N
            for i, (lo, hi, gates) in enumerate(PARTS):
                if stop(T, topo, carriers(T, topo, s)[i], r, gates) == core:
                    sent += pass_on(g, core, s, r, lo, hi, T, topo)
    for c in range(N):
        if core in adders(T, topo, c):
            add(g, core, c, adders(T, topo, c).index(core), T, topo)
    if sent:
        g.wait_ge(T.sem.sendw, sent)


def weights(T, s, lo, hi):
    return T["wc%d" % s][:, lo:hi].bitcast(dt.uint8), T["wp%d" % s][:, lo:hi]


def carry(g, core, r, i, T, topo):
    lo, hi, gates = PARTS[i]
    nu = on_chip_engines(T, topo, r).bit_count()
    got = nu if i == 0 else nu // 2
    codes, plane = weights(T, r, lo, hi)
    n = 0
    for k in STEPS:
        c = (r + k) % N
        to = stop(T, topo, core, c, gates)
        mask = topo.mask(core, to)
        there = to == T.cores[c]
        g.wait_ge(T.sem.rc, got)
        send(g, topo, to, codes, codes, mask, T.sem[("wa%d" if there else "gc%d") % r], T.sem.sendw)
        g.wait_ge(T.sem.rp, got)
        send(g, topo, to, plane, plane, mask, T.sem[("wa%d" if there else "gp%d") % r], T.sem.sendw)
        n += 2 * mask.bit_count()
    return n


def pass_on(g, core, s, c, lo, hi, T, topo):
    to = T.cores[c]
    mask = topo.mask(core, to)
    n = mask.bit_count()
    codes, plane = weights(T, s, lo, hi)
    g.wait_ge(T.sem["gc%d" % s], n)
    send(g, topo, to, codes, codes, mask, T.sem["wa%d" % s], T.sem.sendw)
    g.wait_ge(T.sem["gp%d" % s], n)
    send(g, topo, to, plane, plane, mask, T.sem["wa%d" % s], T.sem.sendw)
    return 2 * n


def add(g, core, c, i, T, topo):
    to = T.cores[c]
    src = [(c - k) % N for k in STEPS]
    at = [T.land[:, s * NC:(s + 1) * NC] for s in src]
    inc = [part_engines(T, topo, s, core).bit_count() for s in src]
    V = g.vector
    V.wait_ge(T.sem["sa%d" % src[0]], inc[0])
    V.wait_ge(T.sem["sa%d" % src[1]], inc[1])
    V.tensor_tensor(T.pre[:, 0:NC], at[0], at[1], AluOpType.add).then_inc(T.sem.pre, 1)
    V.wait_ge(T.sem.pre, 1)
    V.wait_ge(T.sem["sa%d" % src[2]], inc[2])
    V.tensor_tensor(T.pre[:, NC:2 * NC], T.pre[:, 0:NC], at[2], AluOpType.add).then_inc(T.sem.total, 1)
    g.wait_ge(T.sem.total, 1)
    mask = topo.mask(core, to)
    send(g, topo, to, T.folded[:, i * NC:(i + 1) * NC], T.pre[:, NC:2 * NC], mask, T.sem["fold%d" % i], T.sem.sendf)
    g.wait_ge(T.sem.sendf, mask.bit_count())


def owner(g, core, r, T, topo):
    V, S, P, Y, sem = g.vector, g.scalar, g.tensor, g.sync, T.sem
    order = [(r + k) % N for k in STEPS]
    back = [(r - k) % N for k in STEPS]
    carrier = carriers(T, topo, r)
    off = topo.mask(core, T.cores[order[0]])
    up = on_chip_engines(T, topo, r)
    ne, nu = off.bit_count(), up.bit_count()
    read = [0] * 8

    def slot(name, c, w=NC):
        return T[name][:, c * w:(c + 1) * w]

    def bank(b):
        return T.ps[:, 512 * b:512 * b + NC]

    def product(b, wq, ws, i, xq, xs, start=True, stop=True):
        if start and read[b]:
            P.wait_ge(sem["rd%d" % b], read[b])
        m = P.matmul_mx(bank(b), wq[:, 128 * i:128 * i + 128], ws[:, 128 * i:128 * i + 128], xq, xs, start, stop)
        if stop:
            m.then_inc(sem["mm%d" % b], 1)

    def turn_of(q, b):
        read[b] += 1
        q.wait_ge(sem["mm%d" % b], read[b])
        return b, read[b]

    def act(q, b, out):
        mark = turn_of(q, b)
        if q is S:
            S.activation(out, bank(b), ACT.Relu, scale=C1).then_inc(sem["rd%d" % b], 1)
        else:
            V.tensor_scalar(out, bank(b), 0.0, C1, AluOpType.max, AluOpType.mult).then_inc(sem["rd%d" % b], 1)
        return mark

    def evict(q, b, out):
        mark = turn_of(q, b)
        if q is S:
            S.activation(out, bank(b), ACT.Copy).then_inc(sem["rd%d" % b], 1)
        else:
            V.tensor_copy(out, bank(b)).then_inc(sem["rd%d" % b], 1)
        return mark

    def after(q, marks):
        for b, n in marks:
            q.wait_ge(sem["rd%d" % b], n)

    def acts(name, c, banks, qs):
        return [act(q, b, T[name + "t"][:, 4 * NC * c + i:4 * NC * (c + 1):4]) for i, (q, b) in enumerate(zip(qs, banks))]

    def pack(name, c, marks):
        after(V, marks)
        V.quantize_mx(slot(name + "q", c), slot(name + "s", c), slot(name + "t", c, 4 * NC)).then_inc(sem["q%s%d" % (name, c)], 1)

    wc, wp = T["wc%d" % r], T["wp%d" % r]
    LOW, BOTH = (0, 1, 2, 3), (S, V, S, V)

    Y.dma_start(T.xin[:], T.x[:]).then_inc(sem.lx, 16)
    Y.dma_start(T.w1in[:], T.w1[:]).then_inc(sem.l1, 16)
    Y.dma_start(T.w4in[:], T.w4[:]).then_inc(sem.l4, 16)
    Y.dma_start(T.w3in[:], T.w3[:]).then_inc(sem.l3, 16)
    Y.dma_start(T.w2in[:], T.w2[:]).then_inc(sem.l2, 16)

    V.wait_ge(sem.lx, 16)
    V.quantize_mx(slot("xq", r), slot("xs", r), T.xin[:]).then_inc(sem.qx, 1)

    g.wait_ge(sem.qx, 1)
    xc, xp = slot("xq", r).bitcast(dt.uint8), slot("xs", r)
    for k, v in ((2, xp), (0, xc), (0, xp), (1, xc), (1, xp), (2, xc)):
        send(g, topo, T.cores[back[k]], v, v, off, sem["xa%d" % r], sem.sendx)

    def first(c):
        if c != r:
            P.wait_ge(sem["xa%d" % c], 2 * ne)
        for b in range(4):
            product(b, T.w1q, T.w1s, b, slot("xq", c), slot("xs", c))

    def second(c):
        P.wait_ge(sem["qt%d" % c], 1)
        for b in range(4):
            product(4 + b, T.w2q, T.w2s, b, slot("tq", c), slot("ts", c))

    out = {}

    def take(c):
        out[c] = [evict(q, 4 + b, slot("sp", 4 * c + b)) for b, q in enumerate(BOTH)]

    V.wait_ge(sem.l1, 16)
    V.quantize_mx(T.w1q[:], T.w1s[:], T.w1in[:]).then_inc(sem.q1, 1)
    P.wait_ge(sem.qx, 1)
    P.wait_ge(sem.q1, 1)
    first(r)
    marks = acts("t", r, LOW, (S, S, S, S))
    V.wait_ge(sem.l4, 16)
    V.quantize_mx(wc[:, W3C:], wp[:, W3C:], T.w4in[:]).then_inc(sem.q4, 1)
    V.wait_ge(sem.l3, 16)
    V.quantize_mx(wc[:, 0:W3C], wp[:, 0:W3C], T.w3in[:]).then_inc(sem.q3, 1)
    pack("t", r, marks)
    V.wait_ge(sem.l2, 16)
    V.quantize_mx(T.w2q[:], T.w2s[:], T.w2in[:]).then_inc(sem.q2, 1)

    g.wait_ge(sem.q4, 1)
    for v, s in zip(weights(T, r, *PARTS[0][:2]), (sem.rc, sem.rp)):
        send(g, topo, carrier[0], v, v, up, s, sem.sendw)
    halves = [(c, m, weights(T, r, *p[:2])) for c, m, p in zip(carrier[1:], cut_mask(up, 2), PARTS[1:])]
    g.wait_ge(sem.q3, 1)
    for j, s in enumerate((sem.rc, sem.rp)):
        g.remote_dma_fused([copy(topo, c, v[j], v[j], m, s) for c, m, v in halves], local_sem=sem.sendw)

    c1, c2, c3 = order
    first(c1)
    pack("t", c1, acts("t", c1, LOW, BOTH))
    first(c2)
    P.wait_ge(sem.q2, 1)
    second(c1)
    pack("t", c2, acts("t", c2, LOW, BOTH))
    first(c3)
    take(c1)
    second(c2)
    pack("t", c3, acts("t", c3, LOW, BOTH))
    take(c2)
    second(c3)
    take(c3)
    second(r)

    sent = 0
    for c in order:
        for i, a in enumerate(adders(T, topo, c)):
            after(g, out[c][i:i + 1])
            mask = part_engines(T, topo, r, a)
            send(g, topo, a, slot("land", r), slot("sp", 4 * c + i), mask, sem["sa%d" % r], sem.sends)
            sent += mask.bit_count()
    for c in order:
        after(g, out[c][3:4])
        send(g, topo, T.cores[c], slot("direct", r), slot("sp", 4 * c + 3), off, sem["da%d" % r], sem.sendd)

    Y.wait_ge(sem.sends, sent)
    for c in [r] + order:
        Y.wait_ge(sem["qt%d" % c], 1)
        Y.dma_start(T.t[c], slot("tt", c, 4 * NC)).then_inc(sem.st, 16)

    def mine(b, other, out):
        mark = turn_of(V, 4 + b)
        V.tensor_tensor(out, bank(4 + b), other, AluOpType.add).then_inc(sem["rd%d" % (4 + b)], 1)
        return mark

    def came(k):
        V.wait_ge(sem["da%d" % back[k]], ne)
        return slot("direct", back[k])

    def act_h(b):
        S.activation(T.ht[:, b:4 * NC:4], slot("acc", b), ACT.Relu, scale=C2).then_inc(sem.hact, 1)

    after(V, [mine(3, came(0), slot("part", 0))])
    V.tensor_tensor(slot("part", 1), slot("part", 0), came(1), AluOpType.add).then_inc(sem.add0, 1)
    V.wait_ge(sem.add0, 1)
    V.tensor_tensor(slot("acc", 3), slot("part", 1), came(2), AluOpType.add).then_inc(sem.add1, 1)
    S.wait_ge(sem.add1, 1)
    act_h(3)
    for b in range(ADDED):
        V.wait_ge(sem["fold%d" % b], ne)
        after(S, [mine(b, slot("folded", b), slot("acc", b))])
        act_h(b)
    V.wait_ge(sem.hact, 4)
    V.quantize_mx(T.hq[:], T.hs[:], T.ht[:]).then_inc(sem.qh, 1)
    Y.wait_ge(sem.qh, 1)
    Y.dma_start(T.h[:], T.ht[:]).then_inc(sem.st, 16)

    turn = [r] + back
    z = [0]

    def third(c):
        if c != r:
            P.wait_ge(sem["wa%d" % c], 2 * ne * len(PARTS))
        banks = [(z[0] + b) % 7 for b in range(4)]
        z[0] += 4
        for b in range(4):
            product(banks[b], T["wc%d" % c], T["wp%d" % c], b, T.hq[:], T.hs[:])
        pack("u", c, acts("u", c, banks, BOTH))

    def fourth(c):
        P.wait_ge(sem["qu%d" % c], 1)
        product(7, T["wc%d" % c], T["wp%d" % c], 4, slot("uq", c), slot("us", c), c == turn[0], c == turn[3])

    P.wait_ge(sem.q3, 1)
    P.wait_ge(sem.q4, 1)
    P.wait_ge(sem.qh, 1)
    third(turn[0])
    for k in (1, 2, 3):
        third(turn[k])
        fourth(turn[k - 1])
    fourth(turn[3])
    after(Y, [evict(V, 7, T.yout[:])])
    Y.dma_start(T.y[:], T.yout[:]).then_inc(sem.st, 16)

    Y.wait_ge(sem.st, 6 * 16)
    g.wait_ge(sem.sendx, 6 * ne)
    g.wait_ge(sem.sendw, 4 * nu)
    g.wait_ge(sem.sendd, 3 * ne)
